import numpy as np, ml_dtypes
CORES = [2,10,34,50,74,82,98,114,130,138,162,178,202,210,226,242]
N = 16
F = 64
def setup_inputs(rng):
    return {"x": rng.standard_normal((N, 128, N * F), dtype=np.float32).astype(ml_dtypes.bfloat16), "w": rng.standard_normal((N, 128, 128), dtype=np.float32).astype(ml_dtypes.bfloat16)}
def setup_inputs_big(rng):
    d = setup_inputs(rng)
    for k in ("x", "w"): d[k] = (d[k].astype(np.float32) * 1024.0).astype(d[k].dtype)
    return d
def setup_inputs_small(rng):
    d = setup_inputs(rng)
    for k in ("x", "w"): d[k] = (d[k].astype(np.float32) * (1 / 1024.0)).astype(d[k].dtype)
    return d
def setup_inputs_apart(rng):
    d = setup_inputs(rng)
    f = (10.0 ** rng.permutation(np.linspace(-1.5, 1.5, N))).astype(np.float32).reshape(N, 1, 1)
    for k in ("x", "w"): d[k] = (d[k].astype(np.float32) * f).astype(d[k].dtype)
    return d
def reference(x, w):
    X, W = x.astype(np.float64), w.astype(np.float64)
    s = X.sum(axis=0)
    o = np.concatenate([W[r].T @ s[:, F * r:F * r + F] for r in range(N)], axis=1).astype(ml_dtypes.bfloat16 if x.dtype != np.float64 else np.float64)
    return {"y": np.broadcast_to(o, (N,) + o.shape)}

@@ -1,0 +1,184 @@
+from concourse.bass import DstId, RemoteDMATransfer
+
+N, F, P = 16, 64, 128
+S = 4
+B = N // S
+WORLD = 256
+
+SCRATCH = {
+    "X": ("sbuf", [P, N * F], "bfloat16"),
+    "W": ("sbuf", [P, P], "bfloat16"),
+    "R": ("sbuf", [P, N * F], "bfloat16"),
+    "Y": ("sbuf", [P, N * F], "bfloat16"),
+    "ACC": ("psum", [P, F], "float32"),
+}
+SEMAPHORES = (["ld%d" % q for q in range(S)] + ["ldw", "hx", "hy", "mm", "cp", "snd", "st"]
+              + ["a%d" % i for i in range(N)] + ["y%d" % q for q in range(S)])
+
+
+def blk(i):
+    return slice(i * F, (i + 1) * F)
+
+
+def slc(q):
+    return slice(q * B * F, (q + 1) * B * F)
+
+
+def engines(mask):
+    return [e for e in range(16) if (mask >> e) & 1]
+
+
+def bits(es):
+    m = 0
+    for e in es:
+        m |= 1 << e
+    return m
+
+
+def deal(mask, shares):
+    es, out = engines(mask), []
+    for n in shares:
+        out.append(bits(es[:n]))
+        es = es[n:]
+    return out
+
+
+def team_of(rc, cores, topo):
+    chip = [c for c in range(WORLD) if topo.host(c) == topo.host(rc) and topo.chip(c) == topo.chip(rc)]
+    free = [c for c in chip if c not in cores and all(topo.may_write(c, d) for d in cores)]
+    free.sort(key=lambda c: (topo.die(c) != topo.die(rc), c))
+    return [rc] + free[:S - 1]
+
+
+def peers(i, m):
+    q = (i // B + m) % S
+    return [d for d in range(q * B, (q + 1) * B) if d != i]
+
+
+def scatter_masks(src, ds, cores, topo):
+    common = topo.mask(src, cores[ds[0]])
+    for d in ds:
+        common &= topo.mask(src, cores[d])
+    n = len(engines(common))
+    share = 1
+    while share * 2 * len(ds) <= n:
+        share *= 2
+    shares = [share] * len(ds)
+    left = n - share * len(ds)
+    for k in range(len(ds)):
+        if left >= shares[k]:
+            left -= shares[k]
+            shares[k] *= 2
+    return deal(common, shares), common
+
+
+def dst_id(topo, dst, src):
+    rid, pid = topo.addr(dst, src)
+    return DstId(rid=rid, pnc=pid)
+
+
+def send_scatter(g, T, topo, core, i, m, cores):
+    ds = peers(i, m)
+    masks, _ = scatter_masks(core, ds, cores, topo)
+    g.remote_dma_fused(
+        [RemoteDMATransfer(dst_ids=[dst_id(topo, cores[d], core)], dma_engine_mask=mk, remote_sem=T.sem["a%d" % i],
+                           src=T.X[:, blk(d)], dst=T.R[:, blk(i)]) for d, mk in zip(ds, masks)],
+        local_sem=T.sem.snd)
+    return sum(len(engines(mk)) for mk in masks)
+
+
+def send_gather(g, T, topo, core, i, m, cores):
+    ds = peers(i, m)
+    _, common = scatter_masks(core, ds, cores, topo)
+    g.remote_dma_fused(
+        [RemoteDMATransfer(dst_ids=[dst_id(topo, cores[d], core) for d in ds], dma_engine_mask=common,
+                           remote_sem=T.sem["y%d" % (i // B)], srcs=[T.Y[:, blk(i)]],
+                           dsts=[T.Y[:, blk(i)] for d in ds])],
+        local_sem=T.sem.snd)
+    return len(engines(common))
+
+
+def rank_program(g, core, T, topo):
+    cores = list(T.cores)
+    teams = [team_of(rc, cores, topo) for rc in cores]
+    rank = T.rank_of(core)
+
+    if rank is None:
+        mine = [(i, tm.index(core)) for i, tm in enumerate(teams) if core in tm]
+        if not mine:
+            return
+        i, m = mine[0]
+        rc = cores[i]
+        hand = deal(topo.mask(rc, core), [4] * (S - 1))[m - 1]
+        g.wait_ge(T.sem.hx, len(engines(hand)))
+        sent = send_scatter(g, T, topo, core, i, m, cores)
+        g.wait_ge(T.sem.hy, len(engines(topo.mask(rc, core))))
+        sent += send_gather(g, T, topo, core, i, m, cores)
+        g.wait_ge(T.sem.snd, sent)
+        return
+
+    i, q0, tm = rank, rank // B, teams[rank]
+    qs = [(q0 + m) % S for m in range(S)]
+
+    for k, m in enumerate([1, 2, 3, 0]):
+        queue = g.sync if k % 2 == 0 else g.scalar
+        queue.dma_start(T.X[:, slc(qs[m])], T.x[:, slc(qs[m])]).then_inc(T.sem["ld%d" % qs[m]], 16)
+    g.sync.dma_start(T.W[:, :], T.w[:, :]).then_inc(T.sem.ldw, 16)
+
+    for m in range(1, S):
+        g.wait_ge(T.sem["ld%d" % qs[m]], 16)
+    onchip = topo.mask(core, tm[1])
+    for h in tm[1:]:
+        onchip &= topo.mask(core, h)
+    hand = deal(onchip, [4] * (S - 1))
+    g.remote_dma_fused(
+        [RemoteDMATransfer(dst_ids=[dst_id(topo, tm[m], core)], dma_engine_mask=hand[m - 1], remote_sem=T.sem.hx,
+                           src=T.X[:, slc(qs[m])], dst=T.X[:, slc(qs[m])]) for m in range(1, S)],
+        local_sem=T.sem.snd)
+    sent = sum(len(engines(mk)) for mk in hand)
+
+    g.wait_ge(T.sem["ld%d" % q0], 16)
+    sent += send_scatter(g, T, topo, core, i, 0, cores)
+
+    te = g.tensor
+    te.wait_ge(T.sem.ldw, 16)
+    te.wait_ge(T.sem["ld%d" % q0], 16)
+    te.matmul(T.ACC[:, :], T.W[:, :], T.X[:, blk(i)], start=True, stop=False)
+    order = []
+    for m in range(S):
+        order += [j for j in range(N) if j != i and (j // B + m) % S == q0]
+    for k, j in enumerate(order):
+        m = (q0 - j // B) % S
+        ds = peers(j, m)
+        masks, _ = scatter_masks(teams[j][m], ds, cores, topo)
+        te.wait_ge(T.sem["a%d" % j], len(engines(masks[ds.index(i)])))
+        mmul = te.matmul(T.ACC[:, :], T.W[:, :], T.R[:, blk(j)], start=False, stop=(k == len(order) - 1))
+    mmul.then_inc(T.sem.mm, 1)
+
+    g.vector.wait_ge(T.sem.mm, 1)
+    g.vector.tensor_copy(T.Y[:, blk(i)], T.ACC[:, :]).then_inc(T.sem.cp, 1)
+    g.wait_ge(T.sem.cp, 1)
+    g.remote_dma_fused(
+        [RemoteDMATransfer(dst_ids=[dst_id(topo, h, core) for h in tm[1:]], dma_engine_mask=onchip,
+                           remote_sem=T.sem.hy, srcs=[T.Y[:, blk(i)]], dsts=[T.Y[:, blk(i)] for h in tm[1:]])],
+        local_sem=T.sem.snd)
+    sent += len(engines(onchip))
+
+    sent += send_gather(g, T, topo, core, i, 0, cores)
+
+    for k, m in enumerate(range(S)):
+        queue = g.sync if k % 2 == 0 else g.scalar
+        q = qs[m]
+        need = 0
+        for j in range(q * B, (q + 1) * B):
+            if j == i:
+                queue.wait_ge(T.sem.cp, 1)
+            else:
+                mj = (q0 - q) % S
+                _, common = scatter_masks(teams[j][mj], peers(j, mj), cores, topo)
+                need += len(engines(common))
+        queue.wait_ge(T.sem["y%d" % q], need)
+        queue.dma_start(T.y[:, slc(q)], T.Y[:, slc(q)]).then_inc(T.sem.st, 16)
+
+    g.wait_ge(T.sem.snd, sent)
+    g.wait_ge(T.sem.st, 16 * S)

@@ -1,8 +1,9 @@
 from concourse.bass import DstId, RemoteDMATransfer
 
 N, F, P = 16, 64, 128
-S = 4
-B = N // S
+K = 2
+NH1, NH2 = 3, 4
+S, B = 4, 4
 WORLD = 256
 
 SCRATCH = {
@@ -12,16 +13,12 @@ SCRATCH = {
     "Y": ("sbuf", [P, N * F], "bfloat16"),
     "ACC": ("psum", [P, F], "float32"),
 }
-SEMAPHORES = (["ld%d" % q for q in range(S)] + ["ldw", "hx", "hy", "mm", "cp", "snd", "st"]
+SEMAPHORES = (["ld%d" % m for m in range(K + 1)] + ["ldw", "hx", "hy", "mm", "cp", "snd", "st"]
               + ["a%d" % i for i in range(N)] + ["y%d" % q for q in range(S)])
 
 
-def blk(i):
-    return slice(i * F, (i + 1) * F)
-
-
-def slc(q):
-    return slice(q * B * F, (q + 1) * B * F)
+def cols(a, b):
+    return slice(a * F, b * F)
 
 
 def engines(mask):
@@ -46,30 +43,32 @@ def deal(mask, shares):
 def team_of(rc, cores, topo):
     chip = [c for c in range(WORLD) if topo.host(c) == topo.host(rc) and topo.chip(c) == topo.chip(rc)]
     free = [c for c in chip if c not in cores and all(topo.may_write(c, d) for d in cores)]
-    free.sort(key=lambda c: (topo.die(c) != topo.die(rc), c))
-    return [rc] + free[:S - 1]
+    free.sort(key=lambda c: (topo.die(c) == topo.die(rc), c))
+    return [rc] + free[:K]
 
 
-def peers(i, m):
-    q = (i // B + m) % S
-    return [d for d in range(q * B, (q + 1) * B) if d != i]
+def run_of(m, nh):
+    n0 = N - 1 - K * nh
+    return (1, 1 + n0) if m == 0 else (1 + n0 + (m - 1) * nh, 1 + n0 + m * nh)
 
 
-def scatter_masks(src, ds, cores, topo):
-    common = topo.mask(src, cores[ds[0]])
-    for d in ds:
-        common &= topo.mask(src, cores[d])
-    n = len(engines(common))
-    share = 1
-    while share * 2 * len(ds) <= n:
-        share *= 2
-    shares = [share] * len(ds)
-    left = n - share * len(ds)
-    for k in range(len(ds)):
-        if left >= shares[k]:
-            left -= shares[k]
-            shares[k] *= 2
-    return deal(common, shares), common
+def away(src, cores, topo):
+    mk = None
+    for d in cores:
+        if d != src:
+            mk = topo.mask(src, d) if mk is None else mk & topo.mask(src, d)
+    return mk
+
+
+def calls_of(m, nh, ne):
+    a, b = run_of(m, nh)
+    out, size = [], ne
+    while size >= 1:
+        if (b - a) & size:
+            out.append([(o, ne // size) for o in range(a, a + size)])
+            a += size
+        size //= 2
+    return out
 
 
 def dst_id(topo, dst, src):
@@ -78,24 +77,28 @@ def dst_id(topo, dst, src):
 
 
 def send_scatter(g, T, topo, core, i, m, cores):
-    ds = peers(i, m)
-    masks, _ = scatter_masks(core, ds, cores, topo)
-    g.remote_dma_fused(
-        [RemoteDMATransfer(dst_ids=[dst_id(topo, cores[d], core)], dma_engine_mask=mk, remote_sem=T.sem["a%d" % i],
-                           src=T.X[:, blk(d)], dst=T.R[:, blk(i)]) for d, mk in zip(ds, masks)],
-        local_sem=T.sem.snd)
-    return sum(len(engines(mk)) for mk in masks)
+    mk = away(core, cores, topo)
+    sent = 0
+    for call in calls_of(m, NH1, len(engines(mk))):
+        masks = deal(mk, [n for _, n in call])
+        g.remote_dma_fused(
+            [RemoteDMATransfer(dst_ids=[dst_id(topo, cores[(i + o) % N], core)], dma_engine_mask=k,
+                               remote_sem=T.sem["a%d" % i], src=T.X[:, cols(o, o + 1)], dst=T.R[:, cols(i, i + 1)])
+             for (o, _), k in zip(call, masks)], local_sem=T.sem.snd)
+        sent += len(engines(mk))
+    return sent
 
 
 def send_gather(g, T, topo, core, i, m, cores):
-    ds = peers(i, m)
-    _, common = scatter_masks(core, ds, cores, topo)
+    mk = away(core, cores, topo)
+    a, b = run_of(m, NH2)
+    if a == b:
+        return 0
     g.remote_dma_fused(
-        [RemoteDMATransfer(dst_ids=[dst_id(topo, cores[d], core) for d in ds], dma_engine_mask=common,
-                           remote_sem=T.sem["y%d" % (i // B)], srcs=[T.Y[:, blk(i)]],
-                           dsts=[T.Y[:, blk(i)] for d in ds])],
-        local_sem=T.sem.snd)
-    return len(engines(common))
+        [RemoteDMATransfer(dst_ids=[dst_id(topo, cores[(i + o) % N], core) for o in range(a, b)], dma_engine_mask=mk,
+                           remote_sem=T.sem["y%d" % (i // B)], srcs=[T.Y[:, cols(i, i + 1)]],
+                           dsts=[T.Y[:, cols(i, i + 1)] for o in range(a, b)])], local_sem=T.sem.snd)
+    return len(engines(mk))
 
 
 def rank_program(g, core, T, topo):
@@ -108,77 +111,87 @@ def rank_program(g, core, T, topo):
         if not mine:
             return
         i, m = mine[0]
-        rc = cores[i]
-        hand = deal(topo.mask(rc, core), [4] * (S - 1))[m - 1]
-        g.wait_ge(T.sem.hx, len(engines(hand)))
-        sent = send_scatter(g, T, topo, core, i, m, cores)
-        g.wait_ge(T.sem.hy, len(engines(topo.mask(rc, core))))
-        sent += send_gather(g, T, topo, core, i, m, cores)
-        g.wait_ge(T.sem.snd, sent)
+        sent = 0
+        if NH1:
+            g.wait_ge(T.sem.hx, len(engines(topo.mask(cores[i], core))) // K)
+            sent += send_scatter(g, T, topo, core, i, m, cores)
+        if NH2:
+            g.wait_ge(T.sem.hy, len(engines(topo.mask(cores[i], core))))
+            sent += send_gather(g, T, topo, core, i, m, cores)
+        if sent:
+            g.wait_ge(T.sem.snd, sent)
         return
 
-    i, q0, tm = rank, rank // B, teams[rank]
-    qs = [(q0 + m) % S for m in range(S)]
-
-    for k, m in enumerate([1, 2, 3, 0]):
-        queue = g.sync if k % 2 == 0 else g.scalar
-        queue.dma_start(T.X[:, slc(qs[m])], T.x[:, slc(qs[m])]).then_inc(T.sem["ld%d" % qs[m]], 16)
-    g.sync.dma_start(T.W[:, :], T.w[:, :]).then_inc(T.sem.ldw, 16)
-
-    for m in range(1, S):
-        g.wait_ge(T.sem["ld%d" % qs[m]], 16)
+    i, tm = rank, teams[rank]
     onchip = topo.mask(core, tm[1])
     for h in tm[1:]:
         onchip &= topo.mask(core, h)
-    hand = deal(onchip, [4] * (S - 1))
-    g.remote_dma_fused(
-        [RemoteDMATransfer(dst_ids=[dst_id(topo, tm[m], core)], dma_engine_mask=hand[m - 1], remote_sem=T.sem.hx,
-                           src=T.X[:, slc(qs[m])], dst=T.X[:, slc(qs[m])]) for m in range(1, S)],
-        local_sem=T.sem.snd)
-    sent = sum(len(engines(mk)) for mk in hand)
 
-    g.wait_ge(T.sem["ld%d" % q0], 16)
+    loaded = {}
+    k = 0
+    for m in (list(range(1, K + 1)) if NH1 else []) + [0]:
+        a, b = run_of(m, NH1)
+        if m == 0:
+            a = 0
+        loaded[m] = 0
+        while a < b:
+            j = (i + a) % N
+            n = min(b - a, N - j)
+            queue = g.sync if k % 2 == 0 else g.scalar
+            queue.dma_start(T.X[:, cols(a, a + n)], T.x[:, cols(j, j + n)]).then_inc(T.sem["ld%d" % m], 16)
+            loaded[m] += 16
+            a += n
+            k += 1
+    g.sync.dma_start(T.W[:, :], T.w[:, :]).then_inc(T.sem.ldw, 16)
+
+    sent = 0
+    if NH1:
+        for m in range(1, K + 1):
+            g.wait_ge(T.sem["ld%d" % m], loaded[m])
+        hand = deal(onchip, [len(engines(onchip)) // K] * K)
+        g.remote_dma_fused(
+            [RemoteDMATransfer(dst_ids=[dst_id(topo, tm[m], core)], dma_engine_mask=hand[m - 1], remote_sem=T.sem.hx,
+                               src=T.X[:, cols(*run_of(m, NH1))], dst=T.X[:, cols(*run_of(m, NH1))])
+             for m in range(1, K + 1)], local_sem=T.sem.snd)
+        sent += len(engines(onchip))
+
+    g.wait_ge(T.sem.ld0, loaded[0])
     sent += send_scatter(g, T, topo, core, i, 0, cores)
 
     te = g.tensor
     te.wait_ge(T.sem.ldw, 16)
-    te.wait_ge(T.sem["ld%d" % q0], 16)
-    te.matmul(T.ACC[:, :], T.W[:, :], T.X[:, blk(i)], start=True, stop=False)
+    te.wait_ge(T.sem.ld0, loaded[0])
+    te.matmul(T.ACC[:, :], T.W[:, :], T.X[:, cols(0, 1)], start=True, stop=False)
+    ne = len(engines(away(core, cores, topo)))
     order = []
-    for m in range(S):
-        order += [j for j in range(N) if j != i and (j // B + m) % S == q0]
-    for k, j in enumerate(order):
-        m = (q0 - j // B) % S
-        ds = peers(j, m)
-        masks, _ = scatter_masks(teams[j][m], ds, cores, topo)
-        te.wait_ge(T.sem["a%d" % j], len(engines(masks[ds.index(i)])))
-        mmul = te.matmul(T.ACC[:, :], T.W[:, :], T.R[:, blk(j)], start=False, stop=(k == len(order) - 1))
+    for m in range(K + 1):
+        for call in calls_of(m, NH1, ne):
+            order += call
+    for k, (o, n) in enumerate(order):
+        j = (i - o) % N
+        te.wait_ge(T.sem["a%d" % j], n)
+        mmul = te.matmul(T.ACC[:, :], T.W[:, :], T.R[:, cols(j, j + 1)], start=False, stop=(k == len(order) - 1))
     mmul.then_inc(T.sem.mm, 1)
 
     g.vector.wait_ge(T.sem.mm, 1)
-    g.vector.tensor_copy(T.Y[:, blk(i)], T.ACC[:, :]).then_inc(T.sem.cp, 1)
+    g.vector.tensor_copy(T.Y[:, cols(i, i + 1)], T.ACC[:, :]).then_inc(T.sem.cp, 1)
     g.wait_ge(T.sem.cp, 1)
-    g.remote_dma_fused(
-        [RemoteDMATransfer(dst_ids=[dst_id(topo, h, core) for h in tm[1:]], dma_engine_mask=onchip,
-                           remote_sem=T.sem.hy, srcs=[T.Y[:, blk(i)]], dsts=[T.Y[:, blk(i)] for h in tm[1:]])],
-        local_sem=T.sem.snd)
-    sent += len(engines(onchip))
+    if NH2:
+        g.remote_dma_fused(
+            [RemoteDMATransfer(dst_ids=[dst_id(topo, h, core) for h in tm[1:]], dma_engine_mask=onchip,
+                               remote_sem=T.sem.hy, srcs=[T.Y[:, cols(i, i + 1)]],
+                               dsts=[T.Y[:, cols(i, i + 1)] for h in tm[1:]])], local_sem=T.sem.snd)
+        sent += len(engines(onchip))
 
     sent += send_gather(g, T, topo, core, i, 0, cores)
 
-    for k, m in enumerate(range(S)):
+    for k in range(S):
         queue = g.sync if k % 2 == 0 else g.scalar
-        q = qs[m]
-        need = 0
-        for j in range(q * B, (q + 1) * B):
-            if j == i:
-                queue.wait_ge(T.sem.cp, 1)
-            else:
-                mj = (q0 - q) % S
-                _, common = scatter_masks(teams[j][mj], peers(j, mj), cores, topo)
-                need += len(engines(common))
-        queue.wait_ge(T.sem["y%d" % q], need)
-        queue.dma_start(T.y[:, slc(q)], T.Y[:, slc(q)]).then_inc(T.sem.st, 16)
+        q = (i // B + k) % S
+        if q == i // B:
+            queue.wait_ge(T.sem.cp, 1)
+        queue.wait_ge(T.sem["y%d" % q], ne * len([j for j in range(q * B, (q + 1) * B) if j != i]))
+        queue.dma_start(T.y[:, cols(q * B, (q + 1) * B)], T.Y[:, cols(q * B, (q + 1) * B)]).then_inc(T.sem.st, 16)
 
     g.wait_ge(T.sem.snd, sent)
     g.wait_ge(T.sem.st, 16 * S)

@@ -1,9 +1,10 @@
 from concourse.bass import DstId, RemoteDMATransfer
 
 N, F, P = 16, 64, 128
-K = 2
-NH1, NH2 = 3, 4
-S, B = 4, 4
+PLAN1 = [[4, 2, 2, 1], [2, 1], [2], [1]]
+SH1 = [sum(p) for p in PLAN1]
+SH2 = [6, 4, 3, 2]
+K = len(SH1) - 1
 WORLD = 256
 
 SCRATCH = {
@@ -14,7 +15,7 @@ SCRATCH = {
     "ACC": ("psum", [P, F], "float32"),
 }
 SEMAPHORES = (["ld%d" % m for m in range(K + 1)] + ["ldw", "hx", "hy", "mm", "cp", "snd", "st"]
-              + ["a%d" % i for i in range(N)] + ["y%d" % q for q in range(S)])
+              + ["a%d" % i for i in range(N)] + ["y%d" % q for q in range(3)])
 
 
 def cols(a, b):
@@ -47,9 +48,20 @@ def team_of(rc, cores, topo):
     return [rc] + free[:K]
 
 
-def run_of(m, nh):
-    n0 = N - 1 - K * nh
-    return (1, 1 + n0) if m == 0 else (1 + n0 + (m - 1) * nh, 1 + n0 + m * nh)
+def run1(m):
+    a = 1 + sum(SH1[:m])
+    return a, a + SH1[m]
+
+
+def classes():
+    return [(0, 1 + SH2[0]), (1 + SH2[0], N - K), (N - K, N)]
+
+
+def peers2(m):
+    if m == 0:
+        return [(0, list(range(1, 1 + SH2[0])))]
+    a = 1 + SH2[0] + sum(SH2[h] - 1 for h in range(1, m))
+    return [(1, list(range(a, a + SH2[m] - 1))), (2, [N - K + m - 1])]
 
 
 def away(src, cores, topo):
@@ -60,14 +72,11 @@ def away(src, cores, topo):
     return mk
 
 
-def calls_of(m, nh, ne):
-    a, b = run_of(m, nh)
-    out, size = [], ne
-    while size >= 1:
-        if (b - a) & size:
-            out.append([(o, ne // size) for o in range(a, a + size)])
-            a += size
-        size //= 2
+def calls_of(m, ne):
+    a, out = run1(m)[0], []
+    for size in PLAN1[m]:
+        out.append([(o, ne // size) for o in range(a, a + size)])
+        a += size
     return out
 
 
@@ -76,29 +85,20 @@ def dst_id(topo, dst, src):
     return DstId(rid=rid, pnc=pid)
 
 
-def send_scatter(g, T, topo, core, i, m, cores):
+def send_scatter(g, T, topo, core, i, call, cores):
     mk = away(core, cores, topo)
-    sent = 0
-    for call in calls_of(m, NH1, len(engines(mk))):
-        masks = deal(mk, [n for _, n in call])
-        g.remote_dma_fused(
-            [RemoteDMATransfer(dst_ids=[dst_id(topo, cores[(i + o) % N], core)], dma_engine_mask=k,
-                               remote_sem=T.sem["a%d" % i], src=T.X[:, cols(o, o + 1)], dst=T.R[:, cols(i, i + 1)])
-             for (o, _), k in zip(call, masks)], local_sem=T.sem.snd)
-        sent += len(engines(mk))
-    return sent
-
-
-def send_gather(g, T, topo, core, i, m, cores):
-    mk = away(core, cores, topo)
-    a, b = run_of(m, NH2)
-    if a == b:
-        return 0
+    masks = deal(mk, [n for _, n in call])
     g.remote_dma_fused(
-        [RemoteDMATransfer(dst_ids=[dst_id(topo, cores[(i + o) % N], core) for o in range(a, b)], dma_engine_mask=mk,
-                           remote_sem=T.sem["y%d" % (i // B)], srcs=[T.Y[:, cols(i, i + 1)]],
-                           dsts=[T.Y[:, cols(i, i + 1)] for o in range(a, b)])], local_sem=T.sem.snd)
+        [RemoteDMATransfer(dst_ids=[dst_id(topo, cores[(i + o) % N], core)], dma_engine_mask=k,
+                           remote_sem=T.sem["a%d" % i], src=T.X[:, cols(o, o + 1)], dst=T.R[:, cols(i, i + 1)])
+         for (o, _), k in zip(call, masks)], local_sem=T.sem.snd)
     return len(engines(mk))
+
+
+def gather_transfer(T, topo, core, i, q, offs, cores):
+    return RemoteDMATransfer(dst_ids=[dst_id(topo, cores[(i + o) % N], core) for o in offs],
+                             dma_engine_mask=away(core, cores, topo), remote_sem=T.sem["y%d" % q],
+                             srcs=[T.Y[:, cols(i, i + 1)]], dsts=[T.Y[:, cols(i, i + 1)] for o in offs])
 
 
 def rank_program(g, core, T, topo):
@@ -111,26 +111,31 @@ def rank_program(g, core, T, topo):
         if not mine:
             return
         i, m = mine[0]
+        ne = len(engines(away(core, cores, topo)))
+        nhi = len(engines(topo.mask(cores[i], core) & ~away(cores[i], cores, topo)))
         sent = 0
-        if NH1:
-            g.wait_ge(T.sem.hx, len(engines(topo.mask(cores[i], core))) // K)
-            sent += send_scatter(g, T, topo, core, i, m, cores)
-        if NH2:
-            g.wait_ge(T.sem.hy, len(engines(topo.mask(cores[i], core))))
-            sent += send_gather(g, T, topo, core, i, m, cores)
-        if sent:
-            g.wait_ge(T.sem.snd, sent)
+        g.wait_ge(T.sem.hx, nhi)
+        for call in calls_of(m, ne):
+            sent += send_scatter(g, T, topo, core, i, call, cores)
+        g.wait_ge(T.sem.hy, nhi)
+        for q, offs in peers2(m):
+            if offs:
+                g.remote_dma_fused([gather_transfer(T, topo, core, i, q, offs, cores)], local_sem=T.sem.snd)
+                sent += ne
+        g.wait_ge(T.sem.snd, sent)
         return
 
     i, tm = rank, teams[rank]
-    onchip = topo.mask(core, tm[1])
+    lo = away(core, cores, topo)
+    hi = ~lo
     for h in tm[1:]:
-        onchip &= topo.mask(core, h)
+        hi &= topo.mask(core, h)
+    ne, nhi = len(engines(lo)), len(engines(hi))
 
     loaded = {}
     k = 0
-    for m in (list(range(1, K + 1)) if NH1 else []) + [0]:
-        a, b = run_of(m, NH1)
+    for m in list(range(1, K + 1)) + [0]:
+        a, b = run1(m)
         if m == 0:
             a = 0
         loaded[m] = 0
@@ -142,31 +147,33 @@ def rank_program(g, core, T, topo):
             loaded[m] += 16
             a += n
             k += 1
-    g.sync.dma_start(T.W[:, :], T.w[:, :]).then_inc(T.sem.ldw, 16)
+    (g.sync if k % 2 == 0 else g.scalar).dma_start(T.W[:, :], T.w[:, :]).then_inc(T.sem.ldw, 16)
 
     sent = 0
-    if NH1:
-        for m in range(1, K + 1):
-            g.wait_ge(T.sem["ld%d" % m], loaded[m])
-        hand = deal(onchip, [len(engines(onchip)) // K] * K)
+    for m in range(1, K + 1):
+        g.wait_ge(T.sem["ld%d" % m], loaded[m])
         g.remote_dma_fused(
-            [RemoteDMATransfer(dst_ids=[dst_id(topo, tm[m], core)], dma_engine_mask=hand[m - 1], remote_sem=T.sem.hx,
-                               src=T.X[:, cols(*run_of(m, NH1))], dst=T.X[:, cols(*run_of(m, NH1))])
-             for m in range(1, K + 1)], local_sem=T.sem.snd)
-        sent += len(engines(onchip))
-
+            [RemoteDMATransfer(dst_ids=[dst_id(topo, tm[m], core)], dma_engine_mask=hi, remote_sem=T.sem.hx,
+                               src=T.X[:, cols(*run1(m))], dst=T.X[:, cols(*run1(m))])], local_sem=T.sem.snd)
+        sent += nhi
+    own = calls_of(0, ne)
     g.wait_ge(T.sem.ld0, loaded[0])
-    sent += send_scatter(g, T, topo, core, i, 0, cores)
+    for call in own:
+        sent += send_scatter(g, T, topo, core, i, call, cores)
 
     te = g.tensor
     te.wait_ge(T.sem.ldw, 16)
     te.wait_ge(T.sem.ld0, loaded[0])
     te.matmul(T.ACC[:, :], T.W[:, :], T.X[:, cols(0, 1)], start=True, stop=False)
-    ne = len(engines(away(core, cores, topo)))
-    order = []
-    for m in range(K + 1):
-        for call in calls_of(m, NH1, ne):
-            order += call
+    order, late = [], []
+    for c in own[:-1]:
+        order += c
+    for m in range(1, K + 1):
+        cs = calls_of(m, ne)
+        order += cs[0]
+        for c in cs[1:]:
+            late += c
+    order += late + own[-1]
     for k, (o, n) in enumerate(order):
         j = (i - o) % N
         te.wait_ge(T.sem["a%d" % j], n)
@@ -176,22 +183,27 @@ def rank_program(g, core, T, topo):
     g.vector.wait_ge(T.sem.mm, 1)
     g.vector.tensor_copy(T.Y[:, cols(i, i + 1)], T.ACC[:, :]).then_inc(T.sem.cp, 1)
     g.wait_ge(T.sem.cp, 1)
-    if NH2:
-        g.remote_dma_fused(
-            [RemoteDMATransfer(dst_ids=[dst_id(topo, h, core) for h in tm[1:]], dma_engine_mask=onchip,
-                               remote_sem=T.sem.hy, srcs=[T.Y[:, cols(i, i + 1)]],
-                               dsts=[T.Y[:, cols(i, i + 1)] for h in tm[1:]])], local_sem=T.sem.snd)
-        sent += len(engines(onchip))
 
-    sent += send_gather(g, T, topo, core, i, 0, cores)
+    g.remote_dma_fused(
+        [RemoteDMATransfer(dst_ids=[dst_id(topo, h, core) for h in tm[1:]], dma_engine_mask=hi,
+                           remote_sem=T.sem.hy, srcs=[T.Y[:, cols(i, i + 1)]],
+                           dsts=[T.Y[:, cols(i, i + 1)] for h in tm[1:]])], local_sem=T.sem.snd)
+    q0, offs0 = peers2(0)[0]
+    g.remote_dma_fused([gather_transfer(T, topo, core, i, q0, offs0, cores)], local_sem=T.sem.snd)
+    sent += nhi + ne
 
-    for k in range(S):
-        queue = g.sync if k % 2 == 0 else g.scalar
-        q = (i // B + k) % S
-        if q == i // B:
+    stores = 0
+    for q, (a, b) in enumerate(classes()):
+        queue = g.sync if q % 2 == 0 else g.scalar
+        if a == 0:
             queue.wait_ge(T.sem.cp, 1)
-        queue.wait_ge(T.sem["y%d" % q], ne * len([j for j in range(q * B, (q + 1) * B) if j != i]))
-        queue.dma_start(T.y[:, cols(q * B, (q + 1) * B)], T.Y[:, cols(q * B, (q + 1) * B)]).then_inc(T.sem.st, 16)
+        queue.wait_ge(T.sem["y%d" % q], ne * (b - max(a, 1)))
+        j, left = (i - b + 1) % N, b - a
+        while left:
+            n = min(left, N - j)
+            queue.dma_start(T.y[:, cols(j, j + n)], T.Y[:, cols(j, j + n)]).then_inc(T.sem.st, 16)
+            stores += 16
+            j, left = (j + n) % N, left - n
 
     g.wait_ge(T.sem.snd, sent)
-    g.wait_ge(T.sem.st, 16 * S)
+    g.wait_ge(T.sem.st, stores)

from concourse.bass import DstId, RemoteDMATransfer

N, F, P = 16, 64, 128
PLAN1 = [[4, 2, 2, 1], [2, 1], [2], [1]]
SH1 = [sum(p) for p in PLAN1]
SH2 = [6, 4, 3, 2]
K = len(SH1) - 1
WORLD = 256

SCRATCH = {
    "X": ("sbuf", [P, N * F], "bfloat16"),
    "W": ("sbuf", [P, P], "bfloat16"),
    "R": ("sbuf", [P, N * F], "bfloat16"),
    "Y": ("sbuf", [P, N * F], "bfloat16"),
    "ACC": ("psum", [P, F], "float32"),
}
SEMAPHORES = (["ld%d" % m for m in range(K + 1)] + ["ldw", "hx", "hy", "mm", "cp", "snd", "st"]
              + ["a%d" % i for i in range(N)] + ["y%d" % q for q in range(3)])


def cols(a, b):
    return slice(a * F, b * F)


def engines(mask):
    return [e for e in range(16) if (mask >> e) & 1]


def bits(es):
    m = 0
    for e in es:
        m |= 1 << e
    return m


def deal(mask, shares):
    es, out = engines(mask), []
    for n in shares:
        out.append(bits(es[:n]))
        es = es[n:]
    return out


def team_of(rc, cores, topo):
    chip = [c for c in range(WORLD) if topo.host(c) == topo.host(rc) and topo.chip(c) == topo.chip(rc)]
    free = [c for c in chip if c not in cores and all(topo.may_write(c, d) for d in cores)]
    free.sort(key=lambda c: (topo.die(c) == topo.die(rc), c))
    return [rc] + free[:K]


def run1(m):
    a = 1 + sum(SH1[:m])
    return a, a + SH1[m]


def classes():
    return [(0, 1 + SH2[0]), (1 + SH2[0], N - K), (N - K, N)]


def peers2(m):
    if m == 0:
        return [(0, list(range(1, 1 + SH2[0])))]
    a = 1 + SH2[0] + sum(SH2[h] - 1 for h in range(1, m))
    return [(1, list(range(a, a + SH2[m] - 1))), (2, [N - K + m - 1])]


def away(src, cores, topo):
    mk = None
    for d in cores:
        if d != src:
            mk = topo.mask(src, d) if mk is None else mk & topo.mask(src, d)
    return mk


def calls_of(m, ne):
    a, out = run1(m)[0], []
    for size in PLAN1[m]:
        out.append([(o, ne // size) for o in range(a, a + size)])
        a += size
    return out


def dst_id(topo, dst, src):
    rid, pid = topo.addr(dst, src)
    return DstId(rid=rid, pnc=pid)


def send_scatter(g, T, topo, core, i, call, cores):
    mk = away(core, cores, topo)
    masks = deal(mk, [n for _, n in call])
    g.remote_dma_fused(
        [RemoteDMATransfer(dst_ids=[dst_id(topo, cores[(i + o) % N], core)], dma_engine_mask=k,
                           remote_sem=T.sem["a%d" % i], src=T.X[:, cols(o, o + 1)], dst=T.R[:, cols(i, i + 1)])
         for (o, _), k in zip(call, masks)], local_sem=T.sem.snd)
    return len(engines(mk))


def gather_transfer(T, topo, core, i, q, offs, cores):
    return RemoteDMATransfer(dst_ids=[dst_id(topo, cores[(i + o) % N], core) for o in offs],
                             dma_engine_mask=away(core, cores, topo), remote_sem=T.sem["y%d" % q],
                             srcs=[T.Y[:, cols(i, i + 1)]], dsts=[T.Y[:, cols(i, i + 1)] for o in offs])


def rank_program(g, core, T, topo):
    cores = list(T.cores)
    teams = [team_of(rc, cores, topo) for rc in cores]
    rank = T.rank_of(core)

    if rank is None:
        mine = [(i, tm.index(core)) for i, tm in enumerate(teams) if core in tm]
        if not mine:
            return
        i, m = mine[0]
        ne = len(engines(away(core, cores, topo)))
        nhi = len(engines(topo.mask(cores[i], core) & ~away(cores[i], cores, topo)))
        sent = 0
        g.wait_ge(T.sem.hx, nhi)
        for call in calls_of(m, ne):
            sent += send_scatter(g, T, topo, core, i, call, cores)
        g.wait_ge(T.sem.hy, nhi)
        for q, offs in peers2(m):
            if offs:
                g.remote_dma_fused([gather_transfer(T, topo, core, i, q, offs, cores)], local_sem=T.sem.snd)
                sent += ne
        g.wait_ge(T.sem.snd, sent)
        return

    i, tm = rank, teams[rank]
    lo = away(core, cores, topo)
    hi = ~lo
    for h in tm[1:]:
        hi &= topo.mask(core, h)
    ne, nhi = len(engines(lo)), len(engines(hi))

    loaded = {}
    k = 0
    for m in list(range(1, K + 1)) + [0]:
        a, b = run1(m)
        if m == 0:
            a = 0
        loaded[m] = 0
        while a < b:
            j = (i + a) % N
            n = min(b - a, N - j)
            queue = g.sync if k % 2 == 0 else g.scalar
            queue.dma_start(T.X[:, cols(a, a + n)], T.x[:, cols(j, j + n)]).then_inc(T.sem["ld%d" % m], 16)
            loaded[m] += 16
            a += n
            k += 1
    (g.sync if k % 2 == 0 else g.scalar).dma_start(T.W[:, :], T.w[:, :]).then_inc(T.sem.ldw, 16)

    sent = 0
    for m in range(1, K + 1):
        g.wait_ge(T.sem["ld%d" % m], loaded[m])
        g.remote_dma_fused(
            [RemoteDMATransfer(dst_ids=[dst_id(topo, tm[m], core)], dma_engine_mask=hi, remote_sem=T.sem.hx,
                               src=T.X[:, cols(*run1(m))], dst=T.X[:, cols(*run1(m))])], local_sem=T.sem.snd)
        sent += nhi
    own = calls_of(0, ne)
    g.wait_ge(T.sem.ld0, loaded[0])
    for call in own:
        sent += send_scatter(g, T, topo, core, i, call, cores)

    te = g.tensor
    te.wait_ge(T.sem.ldw, 16)
    te.wait_ge(T.sem.ld0, loaded[0])
    te.matmul(T.ACC[:, :], T.W[:, :], T.X[:, cols(0, 1)], start=True, stop=False)
    order, late = [], []
    for c in own[:-1]:
        order += c
    for m in range(1, K + 1):
        cs = calls_of(m, ne)
        order += cs[0]
        for c in cs[1:]:
            late += c
    order += late + own[-1]
    for k, (o, n) in enumerate(order):
        j = (i - o) % N
        te.wait_ge(T.sem["a%d" % j], n)
        mmul = te.matmul(T.ACC[:, :], T.W[:, :], T.R[:, cols(j, j + 1)], start=False, stop=(k == len(order) - 1))
    mmul.then_inc(T.sem.mm, 1)

    g.vector.wait_ge(T.sem.mm, 1)
    g.vector.tensor_copy(T.Y[:, cols(i, i + 1)], T.ACC[:, :]).then_inc(T.sem.cp, 1)
    g.wait_ge(T.sem.cp, 1)

    g.remote_dma_fused(
        [RemoteDMATransfer(dst_ids=[dst_id(topo, h, core) for h in tm[1:]], dma_engine_mask=hi,
                           remote_sem=T.sem.hy, srcs=[T.Y[:, cols(i, i + 1)]],
                           dsts=[T.Y[:, cols(i, i + 1)] for h in tm[1:]])], local_sem=T.sem.snd)
    q0, offs0 = peers2(0)[0]
    g.remote_dma_fused([gather_transfer(T, topo, core, i, q0, offs0, cores)], local_sem=T.sem.snd)
    sent += nhi + ne

    stores = 0
    for q, (a, b) in enumerate(classes()):
        queue = g.sync if q % 2 == 0 else g.scalar
        if a == 0:
            queue.wait_ge(T.sem.cp, 1)
        queue.wait_ge(T.sem["y%d" % q], ne * (b - max(a, 1)))
        j, left = (i - b + 1) % N, b - a
        while left:
            n = min(left, N - j)
            queue.dma_start(T.y[:, cols(j, j + n)], T.Y[:, cols(j, j + n)]).then_inc(T.sem.st, 16)
            stores += 16
            j, left = (j + n) % N, left - n

    g.wait_ge(T.sem.snd, sent)
    g.wait_ge(T.sem.st, stores)
